import numpy as np
import ml_dtypes


def mxq(x, axis, fmt="e4m3"):
    dtype, down = {"e4m3": (ml_dtypes.float8_e4m3fn, 7), "e5m2": (ml_dtypes.float8_e5m2, 14)}[fmt]
    v = np.moveaxis(np.asarray(x, np.float32).astype(ml_dtypes.bfloat16).astype(np.float64), axis, -1)
    blocks = v.reshape(v.shape[:-1] + (-1, 32))
    amax = np.abs(blocks).max(-1, keepdims=True)
    byte = np.maximum(np.where(amax > 0, np.frexp(amax)[1] - 1 + 127, 0) - down, 1)
    scale = np.exp2(byte - 127.0)
    codes = (blocks / scale).astype(np.float32).astype(dtype).astype(np.float64)
    return np.moveaxis((codes * scale).reshape(v.shape), -1, axis)


WIDE = False


def mx_kscale(k):
    if not WIDE:
        return np.ones(k)
    levels = np.array([10, -10, 5, -5, 0])
    if k % 512:
        return np.exp2(np.random.permutation(np.resize(levels, k // 32))).repeat(32)
    a = np.empty((k // 512, 16))
    for p in range(k // 512):
        a[p, :8] = np.random.permutation(np.resize(levels, 8))
        for g in range(8):
            far = levels[np.abs(levels - a[p, g]) >= 10]
            a[p, g + 8] = far[np.random.randint(len(far))]
    return np.exp2(a.ravel()).repeat(32)


def f64(x):
    return np.asarray(x).astype(np.float64)


def striped(idx):
    return np.tile(idx.reshape(-1, 16).T, (8, 1)).astype(np.uint16)


def unstriped(offs):
    return offs[:16].T.reshape(-1).astype(np.int64)


def silu(v):
    return v / (1.0 + np.exp(-np.maximum(v, -700.0)))


K, T, S, H, N = 512, 4096, 1536, 1024, 256


def setup_inputs():
    n = np.random.standard_normal
    s = mx_kscale(K)[:, None]
    u = mx_kscale(H)
    return {
        "xT": (n((K, T)) * s).astype(np.float32),
        "w1": (n((K, H)) / np.sqrt(K) / s * u).astype(np.float32),
        "w2": (n((H, N)) / np.sqrt(H) / u[:, None]).astype(np.float32),
        "offs": striped(np.random.permutation(T)[:S]),
    }


def reference(xT, w1, w2, offs):
    idx = unstriped(offs)
    xq = mxq(f64(xT)[:, idx], 0, "e4m3")
    h = silu(mxq(f64(w1), 0, "e4m3").T @ xq)
    y = mxq(f64(w2), 0, "e4m3").T @ mxq(h, 0, "e4m3")
    return y

@@ -1,0 +1,187 @@
+from contextlib import ExitStack
+
+import concourse.mybir as mybir
+
+K, T, S, H, N = 512, 4096, 1536, 1024, 256
+FLOPS = 2 * S * (K * H + H * N)
+
+F32 = mybir.dt.float32
+BF16 = mybir.dt.bfloat16
+U32 = mybir.dt.uint32
+U16 = mybir.dt.uint16
+U8 = mybir.dt.uint8
+FP8X4 = mybir.dt.float8_e4m3fn_x4
+MULT, ADD = mybir.AluOpType.mult, mybir.AluOpType.add
+COPY = mybir.ActivationFunctionType.Copy
+SILU = mybir.ActivationFunctionType.Silu
+
+P = 128
+SLICE = 512
+SLICES = S // SLICE
+GROUP = 128
+HALF = 512
+CHUNKS = ((2048, 2048), (2048, 1024, 768, 256))
+
+
+def quantize(nc, codes, scales, rows, c0, c1):
+    nc.vector.quantize_mx(
+        out=codes[:, c0:c1].bitcast(FP8X4), scales=scales[:, c0:c1], in_=rows[:, 4 * c0 : 4 * c1]
+    )
+
+
+def tile_picked_pick_mlp_silu_sub_e_kernel(tc, xT, w1, w2, offs, out):
+    nc = tc.nc
+    with ExitStack() as ctx:
+        keep = ctx.enter_context(tc.tile_pool(name="keep", bufs=1))
+        psum_h = ctx.enter_context(tc.psum_pool(name="psum_h", bufs=5))
+        psum_y = ctx.enter_context(tc.psum_pool(name="psum_y", bufs=3))
+
+        warm = keep.tile([P, 1], F32, name="warm")
+        warm_out = keep.tile([P, 1], F32, name="warm_out")
+        nc.vector.memset(warm[:], 0.0)
+        nc.scalar.activation(warm_out[:], warm[:], SILU)
+
+        w1_rows = w1.rearrange("(p j) c -> p j c", j=4)
+        w1_raw = [keep.tile([P, 4, HALF], F32, name=f"w1_raw{b}") for b in range(2)]
+        nc.sync.dma_start(out=w1_raw[0][:], in_=w1_rows[:, :, 0:HALF])
+        offsets = keep.tile([P, S // 16], U16, name="offsets")
+        x_rows = xT.rearrange("(p u j) t -> u p j t", u=2, j=2)
+        x_raw = []
+        for u in range(2):
+            t0 = 0
+            for i, width in enumerate(CHUNKS[u]):
+                raw = keep.tile([P, 2, width], F32, name=f"x_raw{u}_{i}")
+                nc.sync.dma_start(out=raw[:], in_=x_rows[u][:, :, t0 : t0 + width])
+                x_raw.append((u, t0, width, raw))
+                t0 += width
+                if len(x_raw) == 1:
+                    nc.sync.dma_start(offsets[:], offs)
+        nc.sync.dma_start(out=w1_raw[1][:], in_=w1_rows[:, :, HALF:H])
+        w2_raw = keep.tile([P, 2, 4, N], F32, name="w2_raw")
+        w2_rows = w2.rearrange("(b p j) m -> b p j m", b=2, j=4)
+        for b in range(2):
+            nc.sync.dma_start(out=w2_raw[:, b], in_=w2_rows[b])
+
+        w1_bf = [keep.tile([P, 4 * HALF], BF16, name=f"w1_bf{b}", align_bytes=64) for b in range(2)]
+        w1_codes = [keep.tile([P, HALF], U32, name=f"w1_codes{b}", align_bytes=64) for b in range(2)]
+        w1_scales = [keep.tile([P, HALF], U8, name=f"w1_scales{b}", align_bytes=64) for b in range(2)]
+        w2_bf = [keep.tile([P, 4 * N], BF16, name=f"w2_bf{b}", align_bytes=64) for b in range(2)]
+        w2_codes = [keep.tile([P, N], U32, name=f"w2_codes{b}", align_bytes=64) for b in range(2)]
+        w2_scales = [keep.tile([P, N], U8, name=f"w2_scales{b}", align_bytes=64) for b in range(2)]
+        pairs = [keep.tile([P, 2 * T], BF16, name=f"pairs{u}", align_bytes=64) for u in range(2)]
+        x_bf = [keep.tile([P, 4 * SLICE], BF16, name=f"x_bf{s}", align_bytes=64) for s in range(SLICES)]
+        x_codes = [keep.tile([P, SLICE], U32, name=f"x_codes{s}", align_bytes=64) for s in range(SLICES)]
+        x_scales = [keep.tile([P, SLICE], U8, name=f"x_scales{s}", align_bytes=64) for s in range(SLICES)]
+        h_bf = [[keep.tile([P, 4 * SLICE], BF16, name=f"h_bf{s}_{b}", align_bytes=64) for b in range(2)] for s in range(SLICES)]
+        h_codes = [[keep.tile([P, SLICE], U32, name=f"h_codes{s}_{b}", align_bytes=64) for b in range(2)] for s in range(SLICES)]
+        h_scales = [[keep.tile([P, SLICE], U8, name=f"h_scales{s}_{b}", align_bytes=64) for b in range(2)] for s in range(SLICES)]
+
+        def w1_views(b, m0, m1):
+            dst = w1_bf[b][:].rearrange("p (t m j) -> p m t j", t=4, j=4)[:, m0:m1]
+            src = w1_raw[b][:].rearrange("p j (m t) -> p m t j", t=4)[:, m0:m1]
+            return dst, src
+
+        def x_views(u, t0, raw, a, b):
+            dst = pairs[u][:, 2 * (t0 + a) : 2 * (t0 + b)].rearrange("p (t j) -> p t j", j=2)
+            src = raw[:, :, a:b].rearrange("p j t -> p t j")
+            return dst, src
+
+        def gather(u, s):
+            words = x_bf[s][:].bitcast(U32).rearrange("p (n u) -> p n u", u=2)
+            window = pairs[u][:].bitcast(U32)
+            nc.vector.tensor_copy(words[:, :, u], window.indirect(offsets[:, 32 * s : 32 * (s + 1)]))
+
+        def hidden(s, b, g):
+            bank = psum_h.tile([P, 4, GROUP], F32, name="bank_h")
+            cols = slice(GROUP * g, GROUP * (g + 1))
+            for t in range(4):
+                w_cols = slice(P * t, P * (t + 1))
+                nc.tensor.matmul_mx(
+                    out=bank[:, t, :],
+                    lhsT=w1_codes[b][:, w_cols].bitcast(FP8X4), lhsT_scale=w1_scales[b][:, w_cols],
+                    rhs=x_codes[s][:, cols].bitcast(FP8X4), rhs_scale=x_scales[s][:, cols],
+                    start=True, stop=True,
+                )
+            nc.scalar.activation(
+                h_bf[s][b][:, 4 * GROUP * g : 4 * GROUP * (g + 1)].rearrange("p (n t) -> p n t", t=4),
+                bank[:].rearrange("p t n -> p n t"),
+                SILU,
+            )
+
+        def second(s, mt, n0, n1, dst):
+            for b in range(2):
+                nc.tensor.matmul_mx(
+                    out=dst,
+                    lhsT=w2_codes[b][:, P * mt : P * (mt + 1)].bitcast(FP8X4), lhsT_scale=w2_scales[b][:, P * mt : P * (mt + 1)],
+                    rhs=h_codes[s][b][:, n0:n1].bitcast(FP8X4), rhs_scale=h_scales[s][b][:, n0:n1],
+                    start=(b == 0), stop=(b == 1),
+                )
+
+        nc.scalar.activation(*w1_views(0, 0, 128), COPY)
+        quantize(nc, w1_codes[0], w1_scales[0], w1_bf[0], 0, HALF)
+        for i, (u, t0, width, raw) in enumerate(x_raw):
+            last = i == len(x_raw) - 1
+            cut = width * (11 if last else 6 if u == 0 else 9) // 16
+            nc.vector.tensor_copy(*x_views(u, t0, raw, 0, cut))
+            for a in range(cut, width, 640):
+                nc.scalar.activation(*x_views(u, t0, raw, a, min(a + 640, width)), COPY)
+            if u == 1 and not last:
+                gather(0, i - 2)
+
+        gather(1, 0)
+        quantize(nc, x_codes[0], x_scales[0], x_bf[0], 0, 128)
+        quantize(nc, x_codes[0], x_scales[0], x_bf[0], 128, 512 - 128)
+        quantize(nc, x_codes[0], x_scales[0], x_bf[0], 384, 512)
+        for g in range(4):
+            hidden(0, 0, g)
+        gather(1, 1)
+        quantize(nc, x_codes[1], x_scales[1], x_bf[1], 0, 512)
+        for g in range(4):
+            hidden(1, 0, g)
+        for m0 in (0, 32):
+            nc.gpsimd.tensor_scalar(*w1_views(1, m0, m0 + 32), 1.0, 0.0, MULT, ADD)
+        nc.vector.tensor_copy(*w1_views(1, 64, 128))
+        for b in range(2):
+            nc.gpsimd.tensor_scalar(
+                w2_bf[b][:].rearrange("p (m j) -> p m j", j=4), w2_raw[:, b].rearrange("p j m -> p m j"), 1.0, 0.0, MULT, ADD
+            )
+        quantize(nc, w1_codes[1], w1_scales[1], w1_bf[1], 0, HALF)
+        gather(1, 2)
+        quantize(nc, x_codes[2], x_scales[2], x_bf[2], 0, 512)
+        quantize(nc, h_codes[0][0], h_scales[0][0], h_bf[0][0], 0, 512)
+        for g in range(4):
+            hidden(0, 1, g)
+        for b in range(2):
+            quantize(nc, w2_codes[b], w2_scales[b], w2_bf[b], 0, N)
+        quantize(nc, h_codes[1][0], h_scales[1][0], h_bf[1][0], 0, 512)
+        quantize(nc, h_codes[0][1], h_scales[0][1], h_bf[0][1], 0, 512)
+        for g in range(4):
+            hidden(1, 1, g)
+
+        def finish(s):
+            for mt in range(2):
+                bank = psum_y.tile([P, 512], F32, name="bank_y")
+                second(s, mt, 0, 512, bank[:])
+                y = keep.tile([P, 512], F32, name=f"y{s}_{mt}")
+                nc.vector.tensor_copy(y[:], bank[:])
+                nc.sync.dma_start(out=out[P * mt : P * (mt + 1), SLICE * s : SLICE * (s + 1)], in_=y[:])
+
+        finish(0)
+        quantize(nc, h_codes[1][1], h_scales[1][1], h_bf[1][1], 0, 512)
+        for g in range(4):
+            hidden(2, 0, g)
+        finish(1)
+        quantize(nc, h_codes[2][0], h_scales[2][0], h_bf[2][0], 0, 512)
+        for g in range(4):
+            hidden(2, 1, g)
+        for n0, n1 in ((0, 256), (256, 384), (384, 512)):
+            quantize(nc, h_codes[2][1], h_scales[2][1], h_bf[2][1], n0, n1)
+            for mt in range(2):
+                bank = psum_y.tile([P, n1 - n0], F32, name="bank_y")
+                second(2, mt, n0, n1, bank[:])
+                y = keep.tile([P, n1 - n0], F32, name=f"y2_{n0}_{mt}")
+                if mt == 1 and n1 == 512:
+                    nc.scalar.copy(y[:], bank[:])
+                else:
+                    nc.vector.tensor_copy(y[:], bank[:])
+                nc.sync.dma_start(out=out[P * mt : P * (mt + 1), 2 * SLICE + n0 : 2 * SLICE + n1], in_=y[:])

@@ -11,7 +11,6 @@ U32 = mybir.dt.uint32
 U16 = mybir.dt.uint16
 U8 = mybir.dt.uint8
 FP8X4 = mybir.dt.float8_e4m3fn_x4
-MULT, ADD = mybir.AluOpType.mult, mybir.AluOpType.add
 COPY = mybir.ActivationFunctionType.Copy
 SILU = mybir.ActivationFunctionType.Silu
 
@@ -128,6 +127,8 @@ def tile_picked_pick_mlp_silu_sub_e_kernel(tc, xT, w1, w2, offs, out):
             if u == 1 and not last:
                 gather(0, i - 2)
 
+        for m0 in (0, 32):
+            nc.scalar.activation(*w1_views(1, m0, m0 + 32), COPY)
         gather(1, 0)
         quantize(nc, x_codes[0], x_scales[0], x_bf[0], 0, 128)
         quantize(nc, x_codes[0], x_scales[0], x_bf[0], 128, 512 - 128)
@@ -138,19 +139,17 @@ def tile_picked_pick_mlp_silu_sub_e_kernel(tc, xT, w1, w2, offs, out):
         quantize(nc, x_codes[1], x_scales[1], x_bf[1], 0, 512)
         for g in range(4):
             hidden(1, 0, g)
-        for m0 in (0, 32):
-            nc.gpsimd.tensor_scalar(*w1_views(1, m0, m0 + 32), 1.0, 0.0, MULT, ADD)
         nc.vector.tensor_copy(*w1_views(1, 64, 128))
-        for b in range(2):
-            nc.gpsimd.tensor_scalar(
-                w2_bf[b][:].rearrange("p (m j) -> p m j", j=4), w2_raw[:, b].rearrange("p j m -> p m j"), 1.0, 0.0, MULT, ADD
-            )
         quantize(nc, w1_codes[1], w1_scales[1], w1_bf[1], 0, HALF)
         gather(1, 2)
         quantize(nc, x_codes[2], x_scales[2], x_bf[2], 0, 512)
         quantize(nc, h_codes[0][0], h_scales[0][0], h_bf[0][0], 0, 512)
         for g in range(4):
             hidden(0, 1, g)
+        for b in range(2):
+            nc.vector.tensor_copy(
+                w2_bf[b][:].rearrange("p (m j) -> p m j", j=4), w2_raw[:, b].rearrange("p j m -> p m j")
+            )
         for b in range(2):
             quantize(nc, w2_codes[b], w2_scales[b], w2_bf[b], 0, N)
         quantize(nc, h_codes[1][0], h_scales[1][0], h_bf[1][0], 0, 512)

@@ -19,6 +19,7 @@ SLICE = 512
 SLICES = S // SLICE
 GROUP = 128
 HALF = 512
+RUN = 4
 CHUNKS = ((2048, 2048), (2048, 1024, 768, 256))
 
 
@@ -49,21 +50,31 @@ def tile_picked_pick_mlp_silu_sub_e_kernel(tc, xT, w1, w2, offs, out):
         for u in range(2):
             t0 = 0
             for i, width in enumerate(CHUNKS[u]):
-                raw = keep.tile([P, 2, width], F32, name=f"x_raw{u}_{i}")
+                raw = keep.tile([P, 2, width], F32, name=f"x_raw{u}_{i}", align_bytes=64)
                 nc.sync.dma_start(out=raw[:], in_=x_rows[u][:, :, t0 : t0 + width])
                 x_raw.append((u, t0, width, raw))
                 t0 += width
                 if len(x_raw) == 1:
                     nc.sync.dma_start(offsets[:], offs)
-        nc.sync.dma_start(out=w1_raw[1][:], in_=w1_rows[:, :, HALF:H])
+        for c0 in (0, 256):
+            nc.sync.dma_start(out=w1_raw[1][:, :, c0 : c0 + 256], in_=w1_rows[:, :, HALF + c0 : HALF + c0 + 256])
         w2_raw = keep.tile([P, 2, 4, N], F32, name="w2_raw")
-        w2_rows = w2.rearrange("(b p j) m -> b p j m", b=2, j=4)
+        w2_rows = w2.rearrange("(b a t r) m -> b r a t m", b=2, t=4, r=RUN)
         for b in range(2):
-            nc.sync.dma_start(out=w2_raw[:, b], in_=w2_rows[b])
+            for r in range(RUN):
+                nc.sync.dma_start(out=w2_raw[r:P:RUN, b], in_=w2_rows[b, r])
 
         w1_bf = [keep.tile([P, 4 * HALF], BF16, name=f"w1_bf{b}", align_bytes=64) for b in range(2)]
-        w1_codes = [keep.tile([P, HALF], U32, name=f"w1_codes{b}", align_bytes=64) for b in range(2)]
-        w1_scales = [keep.tile([P, HALF], U8, name=f"w1_scales{b}", align_bytes=64) for b in range(2)]
+        w1_codes = [[], []]
+        w1_scales = [[], []]
+
+        def quantize_w1(b, t, tiles, name):
+            codes = keep.tile([P, P * tiles], U32, name=name, align_bytes=64)
+            scales = keep.tile([P, P * tiles], U8, name=f"w1_scales{b}_{t}", align_bytes=64)
+            quantize(nc, codes, scales, w1_bf[b][:, 4 * P * t : 4 * P * (t + tiles)], 0, P * tiles)
+            for i in range(tiles):
+                w1_codes[b].append(codes[:, P * i : P * (i + 1)])
+                w1_scales[b].append(scales[:, P * i : P * (i + 1)])
         w2_bf = [keep.tile([P, 4 * N], BF16, name=f"w2_bf{b}", align_bytes=64) for b in range(2)]
         w2_codes = [keep.tile([P, N], U32, name=f"w2_codes{b}", align_bytes=64) for b in range(2)]
         w2_scales = [keep.tile([P, N], U8, name=f"w2_scales{b}", align_bytes=64) for b in range(2)]
@@ -75,9 +86,9 @@ def tile_picked_pick_mlp_silu_sub_e_kernel(tc, xT, w1, w2, offs, out):
         h_codes = [[keep.tile([P, SLICE], U32, name=f"h_codes{s}_{b}", align_bytes=64) for b in range(2)] for s in range(SLICES)]
         h_scales = [[keep.tile([P, SLICE], U8, name=f"h_scales{s}_{b}", align_bytes=64) for b in range(2)] for s in range(SLICES)]
 
-        def w1_views(b, m0, m1):
-            dst = w1_bf[b][:].rearrange("p (t m j) -> p m t j", t=4, j=4)[:, m0:m1]
-            src = w1_raw[b][:].rearrange("p j (m t) -> p m t j", t=4)[:, m0:m1]
+        def w1_views(b, t, a0, a1):
+            dst = w1_bf[b][:].rearrange("p (t a r j) -> p t a r j", t=4, r=RUN, j=4)[:, t, a0:a1]
+            src = w1_raw[b][:].rearrange("p j (a t r) -> p t a r j", t=4, r=RUN)[:, t, a0:a1]
             return dst, src
 
         def x_views(u, t0, raw, a, b):
@@ -94,10 +105,9 @@ def tile_picked_pick_mlp_silu_sub_e_kernel(tc, xT, w1, w2, offs, out):
             bank = psum_h.tile([P, 4, GROUP], F32, name="bank_h")
             cols = slice(GROUP * g, GROUP * (g + 1))
             for t in range(4):
-                w_cols = slice(P * t, P * (t + 1))
                 nc.tensor.matmul_mx(
                     out=bank[:, t, :],
-                    lhsT=w1_codes[b][:, w_cols].bitcast(FP8X4), lhsT_scale=w1_scales[b][:, w_cols],
+                    lhsT=w1_codes[b][t].bitcast(FP8X4), lhsT_scale=w1_scales[b][t],
                     rhs=x_codes[s][:, cols].bitcast(FP8X4), rhs_scale=x_scales[s][:, cols],
                     start=True, stop=True,
                 )
@@ -116,71 +126,80 @@ def tile_picked_pick_mlp_silu_sub_e_kernel(tc, xT, w1, w2, offs, out):
                     start=(b == 0), stop=(b == 1),
                 )
 
-        nc.scalar.activation(*w1_views(0, 0, 128), COPY)
-        quantize(nc, w1_codes[0], w1_scales[0], w1_bf[0], 0, HALF)
+        for t in range(4):
+            nc.scalar.activation(*w1_views(0, t, 0, 32), COPY)
+        quantize_w1(0, 0, 2, "w1_codes0_0")
         for i, (u, t0, width, raw) in enumerate(x_raw):
             last = i == len(x_raw) - 1
             cut = width * (11 if last else 6 if u == 0 else 9) // 16
             nc.vector.tensor_copy(*x_views(u, t0, raw, 0, cut))
             for a in range(cut, width, 640):
                 nc.scalar.activation(*x_views(u, t0, raw, a, min(a + 640, width)), COPY)
-            if u == 1 and not last:
-                gather(0, i - 2)
+            if i == 1:
+                for s in range(SLICES):
+                    gather(0, s)
 
-        for m0 in (0, 32):
-            nc.scalar.activation(*w1_views(1, m0, m0 + 32), COPY)
-        gather(1, 0)
-        quantize(nc, x_codes[0], x_scales[0], x_bf[0], 0, 128)
-        quantize(nc, x_codes[0], x_scales[0], x_bf[0], 128, 512 - 128)
-        quantize(nc, x_codes[0], x_scales[0], x_bf[0], 384, 512)
-        for g in range(4):
-            hidden(0, 0, g)
-        gather(1, 1)
-        quantize(nc, x_codes[1], x_scales[1], x_bf[1], 0, 512)
-        for g in range(4):
-            hidden(1, 0, g)
-        nc.vector.tensor_copy(*w1_views(1, 64, 128))
-        quantize(nc, w1_codes[1], w1_scales[1], w1_bf[1], 0, HALF)
-        gather(1, 2)
-        quantize(nc, x_codes[2], x_scales[2], x_bf[2], 0, 512)
-        quantize(nc, h_codes[0][0], h_scales[0][0], h_bf[0][0], 0, 512)
-        for g in range(4):
-            hidden(0, 1, g)
-        for b in range(2):
-            nc.vector.tensor_copy(
-                w2_bf[b][:].rearrange("p (m j) -> p m j", j=4), w2_raw[:, b].rearrange("p j m -> p m j")
-            )
-        for b in range(2):
-            quantize(nc, w2_codes[b], w2_scales[b], w2_bf[b], 0, N)
-        quantize(nc, h_codes[1][0], h_scales[1][0], h_bf[1][0], 0, 512)
-        quantize(nc, h_codes[0][1], h_scales[0][1], h_bf[0][1], 0, 512)
-        for g in range(4):
-            hidden(1, 1, g)
+        def w2_views(b):
+            return w2_bf[b][:].rearrange("p (m j) -> p m j", j=4), w2_raw[:, b].rearrange("p j m -> p m j")
 
-        def finish(s):
-            for mt in range(2):
-                bank = psum_y.tile([P, 512], F32, name="bank_y")
-                second(s, mt, 0, 512, bank[:])
-                y = keep.tile([P, 512], F32, name=f"y{s}_{mt}")
-                nc.vector.tensor_copy(y[:], bank[:])
-                nc.sync.dma_start(out=out[P * mt : P * (mt + 1), SLICE * s : SLICE * (s + 1)], in_=y[:])
-
-        finish(0)
-        quantize(nc, h_codes[1][1], h_scales[1][1], h_bf[1][1], 0, 512)
-        for g in range(4):
-            hidden(2, 0, g)
-        finish(1)
-        quantize(nc, h_codes[2][0], h_scales[2][0], h_bf[2][0], 0, 512)
-        for g in range(4):
-            hidden(2, 1, g)
-        for n0, n1 in ((0, 256), (256, 384), (384, 512)):
-            quantize(nc, h_codes[2][1], h_scales[2][1], h_bf[2][1], n0, n1)
+        for t in range(4):
+            nc.scalar.activation(*w1_views(1, t, 0, 16), COPY)
+        def finish(s, n0, n1, engines):
             for mt in range(2):
                 bank = psum_y.tile([P, n1 - n0], F32, name="bank_y")
-                second(2, mt, n0, n1, bank[:])
-                y = keep.tile([P, n1 - n0], F32, name=f"y2_{n0}_{mt}")
-                if mt == 1 and n1 == 512:
+                second(s, mt, n0, n1, bank[:])
+                y = keep.tile([P, n1 - n0], F32, name=f"y{s}_{n0}_{mt}")
+                if engines[mt] == "scalar":
                     nc.scalar.copy(y[:], bank[:])
                 else:
                     nc.vector.tensor_copy(y[:], bank[:])
-                nc.sync.dma_start(out=out[P * mt : P * (mt + 1), 2 * SLICE + n0 : 2 * SLICE + n1], in_=y[:])
+                nc.sync.dma_start(out=out[P * mt : P * (mt + 1), SLICE * s + n0 : SLICE * s + n1], in_=y[:])
+
+        def hiddens(s, b):
+            for g in range(4):
+                hidden(s, b, g)
+
+        def quantize_x(s, c0, c1):
+            quantize(nc, x_codes[s], x_scales[s], x_bf[s], c0, c1)
+
+        def quantize_h(s, b, c0, c1):
+            quantize(nc, h_codes[s][b], h_scales[s][b], h_bf[s][b], c0, c1)
+
+        def quantize_w2(b):
+            quantize(nc, w2_codes[b], w2_scales[b], w2_bf[b], 0, N)
+
+        gather(1, 0)
+        quantize_w1(0, 2, 2, "x_raw1_3")
+        quantize_x(0, 0, 128)
+        for t in (0, 1):
+            nc.vector.tensor_copy(*w1_views(1, t, 16, 32))
+        quantize_x(0, 128, 256)
+        for t in (2, 3):
+            nc.vector.tensor_copy(*w1_views(1, t, 16, 32))
+        quantize_x(0, 256, 384)
+        quantize_x(0, 384, 512)
+        hiddens(0, 0)
+        quantize_w1(1, 0, 4, "w1_codes1_0")
+        hiddens(0, 1)
+        gather(1, 1)
+        nc.vector.tensor_copy(*w2_views(0))
+        quantize_x(1, 0, 512)
+        hiddens(1, 0)
+        gather(1, 2)
+        quantize_h(0, 0, 0, 512)
+        quantize_x(2, 0, 512)
+        hiddens(1, 1)
+        quantize_h(0, 1, 0, 512)
+        nc.vector.tensor_copy(*w2_views(1))
+        quantize_w2(0)
+        quantize_w2(1)
+        finish(0, 0, 512, ("vector", "vector"))
+        hiddens(2, 0)
+        quantize_h(1, 0, 0, 512)
+        quantize_h(1, 1, 0, 512)
+        hiddens(2, 1)
+        quantize_h(2, 0, 0, 512)
+        finish(1, 0, 512, ("vector", "scalar"))
+        for n0 in (0, 256):
+            quantize_h(2, 1, n0, n0 + 256)
+            finish(2, n0, n0 + 256, ("vector", "scalar"))

@@ -19,7 +19,6 @@ SLICE = 512
 SLICES = S // SLICE
 GROUP = 128
 HALF = 512
-RUN = 4
 CHUNKS = ((2048, 2048), (2048, 1024, 768, 256))
 
 
@@ -56,13 +55,11 @@ def tile_picked_pick_mlp_silu_sub_e_kernel(tc, xT, w1, w2, offs, out):
                 t0 += width
                 if len(x_raw) == 1:
                     nc.sync.dma_start(offsets[:], offs)
-        for c0 in (0, 256):
-            nc.sync.dma_start(out=w1_raw[1][:, :, c0 : c0 + 256], in_=w1_rows[:, :, HALF + c0 : HALF + c0 + 256])
+        nc.sync.dma_start(out=w1_raw[1][:], in_=w1_rows[:, :, HALF:H])
         w2_raw = keep.tile([P, 2, 4, N], F32, name="w2_raw")
-        w2_rows = w2.rearrange("(b a t r) m -> b r a t m", b=2, t=4, r=RUN)
+        w2_rows = w2.rearrange("(b p j) m -> b p j m", b=2, j=4)
         for b in range(2):
-            for r in range(RUN):
-                nc.sync.dma_start(out=w2_raw[r:P:RUN, b], in_=w2_rows[b, r])
+            nc.sync.dma_start(out=w2_raw[:, b], in_=w2_rows[b])
 
         w1_bf = [keep.tile([P, 4 * HALF], BF16, name=f"w1_bf{b}", align_bytes=64) for b in range(2)]
         w1_codes = [[], []]
@@ -86,9 +83,9 @@ def tile_picked_pick_mlp_silu_sub_e_kernel(tc, xT, w1, w2, offs, out):
         h_codes = [[keep.tile([P, SLICE], U32, name=f"h_codes{s}_{b}", align_bytes=64) for b in range(2)] for s in range(SLICES)]
         h_scales = [[keep.tile([P, SLICE], U8, name=f"h_scales{s}_{b}", align_bytes=64) for b in range(2)] for s in range(SLICES)]
 
-        def w1_views(b, t, a0, a1):
-            dst = w1_bf[b][:].rearrange("p (t a r j) -> p t a r j", t=4, r=RUN, j=4)[:, t, a0:a1]
-            src = w1_raw[b][:].rearrange("p j (a t r) -> p t a r j", t=4, r=RUN)[:, t, a0:a1]
+        def w1_views(b, m0, m1):
+            dst = w1_bf[b][:].rearrange("p (t m j) -> p m t j", t=4, j=4)[:, m0:m1]
+            src = w1_raw[b][:].rearrange("p j (m t) -> p m t j", t=4)[:, m0:m1]
             return dst, src
 
         def x_views(u, t0, raw, a, b):
@@ -126,8 +123,7 @@ def tile_picked_pick_mlp_silu_sub_e_kernel(tc, xT, w1, w2, offs, out):
                     start=(b == 0), stop=(b == 1),
                 )
 
-        for t in range(4):
-            nc.scalar.activation(*w1_views(0, t, 0, 32), COPY)
+        nc.scalar.activation(*w1_views(0, 0, 128), COPY)
         quantize_w1(0, 0, 2, "w1_codes0_0")
         for i, (u, t0, width, raw) in enumerate(x_raw):
             last = i == len(x_raw) - 1
@@ -142,8 +138,7 @@ def tile_picked_pick_mlp_silu_sub_e_kernel(tc, xT, w1, w2, offs, out):
         def w2_views(b):
             return w2_bf[b][:].rearrange("p (m j) -> p m j", j=4), w2_raw[:, b].rearrange("p j m -> p m j")
 
-        for t in range(4):
-            nc.scalar.activation(*w1_views(1, t, 0, 16), COPY)
+
         def finish(s, n0, n1, engines):
             for mt in range(2):
                 bank = psum_y.tile([P, n1 - n0], F32, name="bank_y")
@@ -171,34 +166,32 @@ def tile_picked_pick_mlp_silu_sub_e_kernel(tc, xT, w1, w2, offs, out):
         gather(1, 0)
         quantize_w1(0, 2, 2, "x_raw1_3")
         quantize_x(0, 0, 128)
-        for t in (0, 1):
-            nc.vector.tensor_copy(*w1_views(1, t, 16, 32))
         quantize_x(0, 128, 256)
-        for t in (2, 3):
-            nc.vector.tensor_copy(*w1_views(1, t, 16, 32))
+        gather(1, 1)
         quantize_x(0, 256, 384)
         quantize_x(0, 384, 512)
         hiddens(0, 0)
-        quantize_w1(1, 0, 4, "w1_codes1_0")
-        hiddens(0, 1)
-        gather(1, 1)
-        nc.vector.tensor_copy(*w2_views(0))
         quantize_x(1, 0, 512)
         hiddens(1, 0)
         gather(1, 2)
-        quantize_h(0, 0, 0, 512)
+        nc.vector.tensor_copy(*w1_views(1, 0, 64))
         quantize_x(2, 0, 512)
-        hiddens(1, 1)
-        quantize_h(0, 1, 0, 512)
-        nc.vector.tensor_copy(*w2_views(1))
-        quantize_w2(0)
-        quantize_w2(1)
-        finish(0, 0, 512, ("vector", "vector"))
         hiddens(2, 0)
+        nc.vector.tensor_copy(*w1_views(1, 64, 128))
+        quantize_h(0, 0, 0, 512)
+        quantize_w1(1, 0, 4, "w1_codes1_0")
+        hiddens(0, 1)
+        for b in range(2):
+            nc.vector.tensor_copy(*w2_views(b))
         quantize_h(1, 0, 0, 512)
+        for b in range(2):
+            quantize_w2(b)
+        quantize_h(2, 0, 0, 512)
+        quantize_h(0, 1, 0, 512)
+        hiddens(1, 1)
+        finish(0, 0, 512, ("vector", "vector"))
         quantize_h(1, 1, 0, 512)
         hiddens(2, 1)
-        quantize_h(2, 0, 0, 512)
         finish(1, 0, 512, ("vector", "scalar"))
         for n0 in (0, 256):
             quantize_h(2, 1, n0, n0 + 256)

from contextlib import ExitStack

import concourse.mybir as mybir

K, T, S, H, N = 512, 4096, 1536, 1024, 256
FLOPS = 2 * S * (K * H + H * N)

F32 = mybir.dt.float32
BF16 = mybir.dt.bfloat16
U32 = mybir.dt.uint32
U16 = mybir.dt.uint16
U8 = mybir.dt.uint8
FP8X4 = mybir.dt.float8_e4m3fn_x4
COPY = mybir.ActivationFunctionType.Copy
SILU = mybir.ActivationFunctionType.Silu

P = 128
SLICE = 512
SLICES = S // SLICE
GROUP = 128
HALF = 512
CHUNKS = ((2048, 2048), (2048, 1024, 768, 256))


def quantize(nc, codes, scales, rows, c0, c1):
    nc.vector.quantize_mx(
        out=codes[:, c0:c1].bitcast(FP8X4), scales=scales[:, c0:c1], in_=rows[:, 4 * c0 : 4 * c1]
    )


def tile_picked_pick_mlp_silu_sub_e_kernel(tc, xT, w1, w2, offs, out):
    nc = tc.nc
    with ExitStack() as ctx:
        keep = ctx.enter_context(tc.tile_pool(name="keep", bufs=1))
        psum_h = ctx.enter_context(tc.psum_pool(name="psum_h", bufs=5))
        psum_y = ctx.enter_context(tc.psum_pool(name="psum_y", bufs=3))

        warm = keep.tile([P, 1], F32, name="warm")
        warm_out = keep.tile([P, 1], F32, name="warm_out")
        nc.vector.memset(warm[:], 0.0)
        nc.scalar.activation(warm_out[:], warm[:], SILU)

        w1_rows = w1.rearrange("(p j) c -> p j c", j=4)
        w1_raw = [keep.tile([P, 4, HALF], F32, name=f"w1_raw{b}") for b in range(2)]
        nc.sync.dma_start(out=w1_raw[0][:], in_=w1_rows[:, :, 0:HALF])
        offsets = keep.tile([P, S // 16], U16, name="offsets")
        x_rows = xT.rearrange("(p u j) t -> u p j t", u=2, j=2)
        x_raw = []
        for u in range(2):
            t0 = 0
            for i, width in enumerate(CHUNKS[u]):
                raw = keep.tile([P, 2, width], F32, name=f"x_raw{u}_{i}", align_bytes=64)
                nc.sync.dma_start(out=raw[:], in_=x_rows[u][:, :, t0 : t0 + width])
                x_raw.append((u, t0, width, raw))
                t0 += width
                if len(x_raw) == 1:
                    nc.sync.dma_start(offsets[:], offs)
        nc.sync.dma_start(out=w1_raw[1][:], in_=w1_rows[:, :, HALF:H])
        w2_raw = keep.tile([P, 2, 4, N], F32, name="w2_raw")
        w2_rows = w2.rearrange("(b p j) m -> b p j m", b=2, j=4)
        for b in range(2):
            nc.sync.dma_start(out=w2_raw[:, b], in_=w2_rows[b])

        w1_bf = [keep.tile([P, 4 * HALF], BF16, name=f"w1_bf{b}", align_bytes=64) for b in range(2)]
        w1_codes = [[], []]
        w1_scales = [[], []]

        def quantize_w1(b, t, tiles, name):
            codes = keep.tile([P, P * tiles], U32, name=name, align_bytes=64)
            scales = keep.tile([P, P * tiles], U8, name=f"w1_scales{b}_{t}", align_bytes=64)
            quantize(nc, codes, scales, w1_bf[b][:, 4 * P * t : 4 * P * (t + tiles)], 0, P * tiles)
            for i in range(tiles):
                w1_codes[b].append(codes[:, P * i : P * (i + 1)])
                w1_scales[b].append(scales[:, P * i : P * (i + 1)])
        w2_bf = [keep.tile([P, 4 * N], BF16, name=f"w2_bf{b}", align_bytes=64) for b in range(2)]
        w2_codes = [keep.tile([P, N], U32, name=f"w2_codes{b}", align_bytes=64) for b in range(2)]
        w2_scales = [keep.tile([P, N], U8, name=f"w2_scales{b}", align_bytes=64) for b in range(2)]
        pairs = [keep.tile([P, 2 * T], BF16, name=f"pairs{u}", align_bytes=64) for u in range(2)]
        x_bf = [keep.tile([P, 4 * SLICE], BF16, name=f"x_bf{s}", align_bytes=64) for s in range(SLICES)]
        x_codes = [keep.tile([P, SLICE], U32, name=f"x_codes{s}", align_bytes=64) for s in range(SLICES)]
        x_scales = [keep.tile([P, SLICE], U8, name=f"x_scales{s}", align_bytes=64) for s in range(SLICES)]
        h_bf = [[keep.tile([P, 4 * SLICE], BF16, name=f"h_bf{s}_{b}", align_bytes=64) for b in range(2)] for s in range(SLICES)]
        h_codes = [[keep.tile([P, SLICE], U32, name=f"h_codes{s}_{b}", align_bytes=64) for b in range(2)] for s in range(SLICES)]
        h_scales = [[keep.tile([P, SLICE], U8, name=f"h_scales{s}_{b}", align_bytes=64) for b in range(2)] for s in range(SLICES)]

        def w1_views(b, m0, m1):
            dst = w1_bf[b][:].rearrange("p (t m j) -> p m t j", t=4, j=4)[:, m0:m1]
            src = w1_raw[b][:].rearrange("p j (m t) -> p m t j", t=4)[:, m0:m1]
            return dst, src

        def x_views(u, t0, raw, a, b):
            dst = pairs[u][:, 2 * (t0 + a) : 2 * (t0 + b)].rearrange("p (t j) -> p t j", j=2)
            src = raw[:, :, a:b].rearrange("p j t -> p t j")
            return dst, src

        def gather(u, s):
            words = x_bf[s][:].bitcast(U32).rearrange("p (n u) -> p n u", u=2)
            window = pairs[u][:].bitcast(U32)
            nc.vector.tensor_copy(words[:, :, u], window.indirect(offsets[:, 32 * s : 32 * (s + 1)]))

        def hidden(s, b, g):
            bank = psum_h.tile([P, 4, GROUP], F32, name="bank_h")
            cols = slice(GROUP * g, GROUP * (g + 1))
            for t in range(4):
                nc.tensor.matmul_mx(
                    out=bank[:, t, :],
                    lhsT=w1_codes[b][t].bitcast(FP8X4), lhsT_scale=w1_scales[b][t],
                    rhs=x_codes[s][:, cols].bitcast(FP8X4), rhs_scale=x_scales[s][:, cols],
                    start=True, stop=True,
                )
            nc.scalar.activation(
                h_bf[s][b][:, 4 * GROUP * g : 4 * GROUP * (g + 1)].rearrange("p (n t) -> p n t", t=4),
                bank[:].rearrange("p t n -> p n t"),
                SILU,
            )

        def second(s, mt, n0, n1, dst):
            for b in range(2):
                nc.tensor.matmul_mx(
                    out=dst,
                    lhsT=w2_codes[b][:, P * mt : P * (mt + 1)].bitcast(FP8X4), lhsT_scale=w2_scales[b][:, P * mt : P * (mt + 1)],
                    rhs=h_codes[s][b][:, n0:n1].bitcast(FP8X4), rhs_scale=h_scales[s][b][:, n0:n1],
                    start=(b == 0), stop=(b == 1),
                )

        nc.scalar.activation(*w1_views(0, 0, 128), COPY)
        quantize_w1(0, 0, 2, "w1_codes0_0")
        for i, (u, t0, width, raw) in enumerate(x_raw):
            last = i == len(x_raw) - 1
            cut = width * (11 if last else 6 if u == 0 else 9) // 16
            nc.vector.tensor_copy(*x_views(u, t0, raw, 0, cut))
            for a in range(cut, width, 640):
                nc.scalar.activation(*x_views(u, t0, raw, a, min(a + 640, width)), COPY)
            if i == 1:
                for s in range(SLICES):
                    gather(0, s)

        def w2_views(b):
            return w2_bf[b][:].rearrange("p (m j) -> p m j", j=4), w2_raw[:, b].rearrange("p j m -> p m j")


        def finish(s, n0, n1, engines):
            for mt in range(2):
                bank = psum_y.tile([P, n1 - n0], F32, name="bank_y")
                second(s, mt, n0, n1, bank[:])
                y = keep.tile([P, n1 - n0], F32, name=f"y{s}_{n0}_{mt}")
                if engines[mt] == "scalar":
                    nc.scalar.copy(y[:], bank[:])
                else:
                    nc.vector.tensor_copy(y[:], bank[:])
                nc.sync.dma_start(out=out[P * mt : P * (mt + 1), SLICE * s + n0 : SLICE * s + n1], in_=y[:])

        def hiddens(s, b):
            for g in range(4):
                hidden(s, b, g)

        def quantize_x(s, c0, c1):
            quantize(nc, x_codes[s], x_scales[s], x_bf[s], c0, c1)

        def quantize_h(s, b, c0, c1):
            quantize(nc, h_codes[s][b], h_scales[s][b], h_bf[s][b], c0, c1)

        def quantize_w2(b):
            quantize(nc, w2_codes[b], w2_scales[b], w2_bf[b], 0, N)

        gather(1, 0)
        quantize_w1(0, 2, 2, "x_raw1_3")
        quantize_x(0, 0, 128)
        quantize_x(0, 128, 256)
        gather(1, 1)
        quantize_x(0, 256, 384)
        quantize_x(0, 384, 512)
        hiddens(0, 0)
        quantize_x(1, 0, 512)
        hiddens(1, 0)
        gather(1, 2)
        nc.vector.tensor_copy(*w1_views(1, 0, 64))
        quantize_x(2, 0, 512)
        hiddens(2, 0)
        nc.vector.tensor_copy(*w1_views(1, 64, 128))
        quantize_h(0, 0, 0, 512)
        quantize_w1(1, 0, 4, "w1_codes1_0")
        hiddens(0, 1)
        for b in range(2):
            nc.vector.tensor_copy(*w2_views(b))
        quantize_h(1, 0, 0, 512)
        for b in range(2):
            quantize_w2(b)
        quantize_h(2, 0, 0, 512)
        quantize_h(0, 1, 0, 512)
        hiddens(1, 1)
        finish(0, 0, 512, ("vector", "vector"))
        quantize_h(1, 1, 0, 512)
        hiddens(2, 1)
        finish(1, 0, 512, ("vector", "scalar"))
        for n0 in (0, 256):
            quantize_h(2, 1, n0, n0 + 256)
            finish(2, n0, n0 + 256, ("vector", "scalar"))
